import numpy as np
import ml_dtypes


def mxq(x, axis, fmt="e4m3"):
    dtype, down = {"e4m3": (ml_dtypes.float8_e4m3fn, 7), "e5m2": (ml_dtypes.float8_e5m2, 14)}[fmt]
    v = np.moveaxis(np.asarray(x, np.float32).astype(ml_dtypes.bfloat16).astype(np.float64), axis, -1)
    blocks = v.reshape(v.shape[:-1] + (-1, 32))
    amax = np.abs(blocks).max(-1, keepdims=True)
    byte = np.maximum(np.where(amax > 0, np.frexp(amax)[1] - 1 + 127, 0) - down, 1)
    scale = np.exp2(byte - 127.0)
    codes = (blocks / scale).astype(np.float32).astype(dtype).astype(np.float64)
    return np.moveaxis((codes * scale).reshape(v.shape), -1, axis)


WIDE = False


def mx_kscale(k, group=512):
    if not WIDE:
        return np.ones(k)
    levels = np.array([10, -10, 5, -5, 0])
    if group != 512:
        return np.exp2(np.random.permutation(np.resize(levels, k // group))).repeat(group)
    if k % 512:
        return np.exp2(np.random.permutation(np.resize(levels, k // 32))).repeat(32)
    a = np.empty((k // 512, 16))
    for p in range(k // 512):
        a[p, :8] = np.random.permutation(np.resize(levels, 8))
        for g in range(8):
            far = levels[np.abs(levels - a[p, g]) >= 10]
            a[p, g + 8] = far[np.random.randint(len(far))]
    return np.exp2(a.ravel()).repeat(32)


def f64(x):
    return np.asarray(x).astype(np.float64)


def striped(idx):
    return np.tile(np.asarray(idx).reshape(-1, 16).T, (8, 1)).astype(np.uint16)


def unstriped(offs):
    return offs[:16].T.reshape(-1).astype(np.int64)


H, KV, D, NQ, N = 4, 1, 128, 512, 512
CAP = 2.0


def setup_inputs():
    n = np.random.standard_normal
    s = mx_kscale(D, 0)[:, None]
    u = mx_kscale(N)
    t = np.random.uniform(0.5, 2.0, N) * u
    v = n((KV, N, 128))
    return {
        "qT": (n((H, D, NQ)) * s * (0.70 / np.sqrt(D))).astype(np.float32),
        "kT": (n((KV, D, N)) / s).astype(np.float32),
        "t": t.reshape(N, 1).astype(np.float32),
        "v": (v / t[:, None]).astype(np.float32),
        "kb": (0.5 * n((N, 1))).astype(np.float32),
        "gn": np.tile(np.random.uniform(0.5, 2.0, 128), (128, 1)).astype(np.float32),
    }


def reference(qT, kT, t, v, kb, gn):
    a = np.repeat(mxq(f64(kT), 1, "e4m3"), H // KV, 0).transpose(0, 2, 1) @ mxq(f64(qT), 1, "e4m3")
    a = a + f64(kb)
    a = CAP * np.tanh(a / CAP)
    p = 1.0 / (1.0 + np.exp(-a))
    w = p * f64(t)
    y = mxq(w, 1, "e4m3").transpose(0, 2, 1) @ np.repeat(mxq(f64(v), 1, "e4m3"), H // KV, 0)
    y = y / 16.0
    y = y / np.sqrt(np.mean(np.square(y), -1, keepdims=True) + 1e-5) * f64(gn)[:1]
    return y

@@ -1,0 +1,305 @@
+from contextlib import ExitStack
+
+import concourse.mybir as mybir
+
+H, D, NQ, N = 4, 128, 512, 512
+FLOPS = 2 * 2 * H * NQ * N * D
+
+F32 = mybir.dt.float32
+BF16 = mybir.dt.bfloat16
+I32 = mybir.dt.int32
+U32 = mybir.dt.uint32
+U8 = mybir.dt.uint8
+FP8X4 = mybir.dt.float8_e4m3fn_x4
+ACT = mybir.ActivationFunctionType
+ALU = mybir.AluOpType
+
+P = 128
+R = 32
+HALF = 256
+EPS = 256 * 1e-5
+GUESS = float(0x5F3759DF - 2**22 - 2**30)
+UNITS = [(0, 0), (0, 1), (1, 0), (2, 0), (1, 1), (3, 0), (2, 1), (3, 1)]
+EARLY = 4
+
+
+def tile_rows_a_sigmoid_kb_cap_onorm_kernel(tc, qT, kT, t, v, kb, gn, out):
+    nc = tc.nc
+    with ExitStack() as ctx:
+        sb = ctx.enter_context(tc.tile_pool(name="sb", bufs=1))
+        ps = ctx.enter_context(tc.psum_pool(name="ps", bufs=1))
+        ctx.enter_context(tc.manual_schedule())
+
+        def tile(name, shape, dtype):
+            return sb.tile(shape, dtype, name=name, align_bytes=64)
+
+        def packed(name, words):
+            return tile(name, [P, words + words // 4], U32)
+
+        def codes(pk, words, rows, c0, n):
+            return pk[rows, c0 : c0 + n].bitcast(FP8X4)
+
+        def scales(pk, words, rows, c0, n):
+            return pk[rows, words + c0 // 4 : words + (c0 + n) // 4].bitcast(U8)
+
+        k_raw = tile("k_raw", [P, 4, N], F32)
+        q_raw = [tile("q_raw%d" % h, [P, 4, HALF], F32) for h in range(2)]
+        v_raw = tile("v_raw", [P, 4, D], F32)
+        kb_sb = tile("kb_sb", [P, 4], F32)
+        t_sb = tile("t_sb", [P, 4], F32)
+        gn_sb = tile("gn_sb", [P, D], F32)
+        q_view = qT.rearrange("h (p j) n -> (h p) j n", j=4)
+        nc.sync.dma_start(out=k_raw[0:R], in_=kT[0].rearrange("(p j) n -> p j n", j=4))
+        nc.scalar.dma_start(out=q_raw[0][:], in_=q_view[:, :, 0:HALF])
+        nc.sync.dma_start(out=kb_sb[:], in_=kb.rearrange("(s r) o -> s (r o)", r=4))
+        nc.sync.dma_start(out=q_raw[1][:], in_=q_view[:, :, HALF:NQ])
+        nc.sync.dma_start(out=t_sb[:], in_=t.rearrange("(s r) o -> s (r o)", r=4))
+        nc.sync.dma_start(out=v_raw[:], in_=v[0].rearrange("(s r) e -> s r e", r=4))
+        nc.sync.dma_start(out=gn_sb[:], in_=gn)
+
+        k_pk = [[packed("k_pk%d_%d" % (g, a), 256) for a in range(2)] for g in range(H)]
+        q_pk = [packed("q_pk%d" % h, 256) for h in range(2)]
+        v_pk = packed("v_pk", 128)
+        for a in range(2):
+            nc.vector.memset(k_pk[0][a][0:R, 256:320].bitcast(I32), 0)
+
+        k_bf = [tile("k_bf%d" % a, [P, 2, P, 4], BF16) for a in range(2)]
+        q_bf = [tile("q_bf%d" % h, [P, HALF * 4], BF16) for h in range(2)]
+        v_bf = tile("v_bf", [P, D * 4], BF16)
+
+        def k_round(a):
+            return dict(
+                out=k_bf[a][0:R].rearrange("p x s j -> p s j x"),
+                in_=k_raw[0:R].rearrange("p j (s r) -> p s j r", r=4)[:, :, :, 2 * a : 2 * a + 2],
+            )
+
+        def interleave(dst, src):
+            return dict(
+                out=dst[:].rearrange("p (c i j) -> p c j i", i=4, j=4),
+                in_=src[:].rearrange("p j (c i) -> p c j i", i=4),
+            )
+
+        def k_quant(r):
+            a, x = divmod(r, 2)
+            rows = slice(0, R)
+            nc.vector.quantize_mx(
+                out=codes(k_pk[0][a], 256, rows, P * x, P),
+                scales=scales(k_pk[0][a], 256, rows, P * x, P),
+                in_=k_bf[a][0:R, x].rearrange("p s j -> p (s j)"),
+            )
+
+        def quant(pk, words, src):
+            rows = slice(0, P)
+            nc.vector.quantize_mx(out=codes(pk, words, rows, 0, words), scales=scales(pk, words, rows, 0, words), in_=src)
+
+        def k_share(g, a):
+            nc.sync.dma_start(out=k_pk[g][a][R * g : R * g + R].bitcast(I32), in_=k_pk[0][a][0:R].bitcast(I32))
+
+        s_bank = [ps.tile([P, 512], F32, name="s_bank%d" % b) for b in range(5)]
+        y_bank = [ps.tile([P, 512], F32, name="y_bank%d" % b) for b in range(3)]
+
+        def bank_of(u, a):
+            g = UNITS[u][0]
+            return s_bank[a] if g == 0 else s_bank[g + 1]
+
+        def y_of(u):
+            return y_bank[(u // 2) % 3][:, HALF * (u % 2) : HALF * (u % 2) + HALF]
+
+        sig1 = [tile("sig1_%d" % u, [P, 4, HALF], F32) for u in range(8)]
+        prob = [[tile("prob%d_%d" % (u, b), [P, 4, P], F32) for b in range(2)] for u in range(8)]
+        w_bf = [[tile("w_bf%d_%d" % (u, b), [P, 4 * P], BF16) for b in range(2)] for u in range(8)]
+        w_pk = [[packed("w_pk%d_%d" % (u, b), 128) for b in range(2)] for u in range(8)]
+        res = [tile("res%d" % u, [P, 2, D], F32) for u in range(8)]
+
+        def fill(u, a):
+            g, h = UNITS[u]
+            rows = slice(R * g, R * g + R)
+            for x in range(2):
+                for b in range(2):
+                    c0 = HALF * x + P * b
+                    nc.tensor.matmul_mx(
+                        out=bank_of(u, a)[:, c0 : c0 + P],
+                        lhsT=codes(k_pk[g][a], 256, rows, P * x, P),
+                        lhsT_scale=scales(k_pk[g][a], 256, rows, P * x, P),
+                        rhs=codes(q_pk[h], 256, rows, P * b, P),
+                        rhs_scale=scales(q_pk[h], 256, rows, P * b, P),
+                        start=True,
+                        stop=True,
+                    )
+
+        def inner(u, a):
+            for x in range(2):
+                r = 2 * a + x
+                nc.scalar.activation(
+                    out=sig1[u][:, r, :], in_=bank_of(u, a)[:, HALF * x : HALF * x + HALF], func=ACT.Sigmoid, bias=kb_sb[:, r : r + 1]
+                )
+
+        def outer(u, b):
+            nc.scalar.activation(out=prob[u][b][:], in_=sig1[u][:, :, P * b : P * b + P], func=ACT.Sigmoid, scale=4.0, bias=-2.0)
+
+        def weigh(u, b):
+            nc.vector.tensor_tensor(
+                out=w_bf[u][b][:].rearrange("p (c i r) -> p c r i", i=4, r=4),
+                in0=prob[u][b][:].rearrange("p r (c i) -> p c r i", i=4),
+                in1=t_sb[:].unsqueeze(1).unsqueeze(3).to_broadcast([P, P // 4, 4, 4]),
+                op=ALU.mult,
+            )
+
+        def w_quant(u, b):
+            quant(w_pk[u][b], 128, w_bf[u][b][:])
+
+        def second(u, b):
+            rows = slice(0, P)
+            nc.tensor.matmul_mx(
+                out=y_of(u)[:, P * b : P * b + P],
+                lhsT=codes(w_pk[u][b], 128, rows, 0, P),
+                lhsT_scale=scales(w_pk[u][b], 128, rows, 0, P),
+                rhs=codes(v_pk, 128, rows, 0, P),
+                rhs_scale=scales(v_pk, 128, rows, 0, P),
+                start=True,
+                stop=True,
+            )
+
+        st_early = tile("st_early", [P, 2 * EARLY, 3], F32)
+        st_late = tile("st_late", [P, 2 * (7 - EARLY), 3], F32)
+
+        def stats(u):
+            st, i = (st_early, u) if u < EARLY else (st_late, u - EARLY)
+            nc.vector.bn_stats(
+                out=st[:, 2 * i : 2 * i + 2, :].rearrange("p b s -> p (b s)"), in_=y_of(u).rearrange("p (b e) -> p e b", b=2)
+            )
+
+        def finish(u, b, rstd):
+            nc.vector.scalar_tensor_tensor(
+                out=res[u][:, b, :], in0=y_of(u)[:, P * b : P * b + P], scalar=rstd, in1=gn_sb[:], op0=ALU.mult, op1=ALU.mult
+            )
+
+        def store(u):
+            g, h = UNITS[u]
+            nc.sync.dma_start(out=out[g, HALF * h : HALF * h + HALF, :].rearrange("(b p) e -> p b e", b=2), in_=res[u][:])
+
+        def small(name, n, dtype=F32):
+            return tile(name, [P, n], dtype)
+
+        ne = 2 * EARLY
+        m2, ms, xh = small("m2", ne), small("ms", ne), small("xh", ne)
+        guess = small("guess", ne, I32)
+        chain = [
+            lambda: nc.vector.tensor_tensor(out=m2[:], in0=st_early[:, :, 1], in1=st_early[:, :, 1], op=ALU.mult),
+            lambda: nc.vector.scalar_tensor_tensor(
+                out=ms[:], in0=st_early[:, :, 2], scalar=1.0 / D, in1=m2[:], op0=ALU.mult, op1=ALU.add
+            ),
+            lambda: nc.vector.tensor_scalar(out=xh[:], in0=ms[:], scalar1=EPS, scalar2=-0.5, op0=ALU.add, op1=ALU.mult),
+            lambda: nc.vector.tensor_scalar(
+                out=guess[:], in0=xh[:].bitcast(I32), scalar1=-0.5, scalar2=GUESS, op0=ALU.mult, op1=ALU.add
+            ),
+        ]
+
+        def newton(i, root):
+            a, b, nxt = small("na%d" % i, ne), small("nb%d" % i, ne), small("nr%d" % i, ne)
+            chain.extend(
+                [
+                    lambda: nc.vector.tensor_tensor(out=a[:], in0=root, in1=root, op=ALU.mult),
+                    lambda: nc.vector.tensor_tensor(out=b[:], in0=a[:], in1=xh[:], op=ALU.mult),
+                    lambda: nc.vector.scalar_tensor_tensor(out=nxt[:], in0=b[:], scalar=1.5, in1=root, op0=ALU.add, op1=ALU.mult),
+                ]
+            )
+            return nxt[:]
+
+        root = guess[:].bitcast(F32)
+        for i in range(3):
+            root = newton(i, root)
+
+        def link():
+            if chain:
+                chain[0]()
+                chain.remove(chain[0])
+
+        nc.vector.tensor_copy(**k_round(0))
+        nc.vector.tensor_copy(**interleave(q_bf[0], q_raw[0]))
+        k_quant(0)
+        k_quant(1)
+        quant(q_pk[0], 256, q_bf[0][:])
+        nc.vector.tensor_copy(**k_round(1))
+        nc.vector.tensor_copy(**interleave(q_bf[1], q_raw[1]))
+        k_quant(2)
+        k_quant(3)
+        quant(q_pk[1], 256, q_bf[1][:])
+        nc.vector.tensor_copy(**interleave(v_bf, v_raw))
+        for g in range(1, H):
+            for a in range(2):
+                k_share(g, a)
+        fill(0, 0)
+        fill(0, 1)
+        inner(0, 0)
+        inner(0, 1)
+        fill(1, 0)
+
+        for u in range(7):
+            if u == 0:
+                outer(0, 0)
+            inner(u + 1, 0)
+            fill(u + 1, 1)
+            if u + 2 < 8:
+                fill(u + 2, 0)
+            if u > 0:
+                second(u - 1, 0)
+                second(u - 1, 1)
+                outer(u, 0)
+            outer(u, 1)
+            inner(u + 1, 1)
+            weigh(u, 0)
+            if u == 0:
+                quant(v_pk, 128, v_bf[:])
+            if u > EARLY:
+                link()
+            if u > 0:
+                stats(u - 1)
+            if u > EARLY:
+                link()
+            weigh(u, 1)
+            for b in range(2):
+                if u >= EARLY:
+                    link()
+                w_quant(u, b)
+            if u >= EARLY:
+                link()
+        for u in range(2):
+            for b in range(2):
+                finish(u, b, root[:, 2 * u + b : 2 * u + b + 1])
+            store(u)
+
+        second(6, 0)
+        second(6, 1)
+        outer(7, 0)
+        outer(7, 1)
+        weigh(7, 0)
+        weigh(7, 1)
+        w_quant(7, 0)
+        w_quant(7, 1)
+        second(7, 0)
+        second(7, 1)
+        nl = 2 * (7 - EARLY)
+        m2l, ssl, rl = small("m2l", nl), small("ssl", nl), small("rl", nl)
+        stats(6)
+        finish(2, 0, root[:, 4:5])
+        nc.vector.tensor_tensor(out=m2l[:], in0=st_late[:, :, 1], in1=st_late[:, :, 1], op=ALU.mult)
+        finish(2, 1, root[:, 5:6])
+        nc.vector.scalar_tensor_tensor(out=ssl[:], in0=m2l[:], scalar=float(D), in1=st_late[:, :, 2], op0=ALU.mult, op1=ALU.add)
+        store(2)
+        finish(3, 0, root[:, 6:7])
+        finish(3, 1, root[:, 7:8])
+        store(3)
+        nc.scalar.activation(out=rl[:], in_=ssl[:], func=ACT.Abs_reciprocal_sqrt, scale=1.0 / D, bias=EPS)
+        ss7, r7 = small("ss7", 2), small("r7", 2)
+        sq = tile("sq", [P, 2, D], F32)
+        for b in range(2):
+            nc.scalar.activation(out=sq[:, b, :], in_=y_of(7)[:, P * b : P * b + P], func=ACT.Square, accum_out=ss7[:, b : b + 1])
+        nc.scalar.activation(out=r7[:], in_=ss7[:], func=ACT.Abs_reciprocal_sqrt, scale=1.0 / D, bias=EPS)
+        for u in range(EARLY, 7):
+            for b in range(2):
+                finish(u, b, rl[:, 2 * (u - EARLY) + b : 2 * (u - EARLY) + b + 1])
+            store(u)
+        for b in range(2):
+            finish(7, b, r7[:, b : b + 1])
+        store(7)

@@ -18,9 +18,11 @@ P = 128
 R = 32
 HALF = 256
 EPS = 256 * 1e-5
-GUESS = float(0x5F3759DF - 2**22 - 2**30)
-UNITS = [(0, 0), (0, 1), (1, 0), (2, 0), (1, 1), (3, 0), (2, 1), (3, 1)]
-EARLY = 4
+GUESS = float(0x5F1FFFF9 - 2**30)
+STEP_A, STEP_K = 2.38924456, 0.703952253
+UNITS = [(0, 0), (0, 1), (1, 0), (2, 0), (1, 1), (3, 0)]
+BLOCKS = [(g, h, b) for g, h in UNITS for b in range(2)] + [(g, 1, b) for b in range(2) for g in (2, 3)]
+EARLY = 3
 
 
 def tile_rows_a_sigmoid_kb_cap_onorm_kernel(tc, qT, kT, t, v, kb, gn, out):
@@ -33,6 +35,9 @@ def tile_rows_a_sigmoid_kb_cap_onorm_kernel(tc, qT, kT, t, v, kb, gn, out):
         def tile(name, shape, dtype):
             return sb.tile(shape, dtype, name=name, align_bytes=64)
 
+        def small(name, n, dtype=F32):
+            return tile(name, [P, n], dtype)
+
         def packed(name, words):
             return tile(name, [P, words + words // 4], U32)
 
@@ -42,264 +47,349 @@ def tile_rows_a_sigmoid_kb_cap_onorm_kernel(tc, qT, kT, t, v, kb, gn, out):
         def scales(pk, words, rows, c0, n):
             return pk[rows, words + c0 // 4 : words + (c0 + n) // 4].bitcast(U8)
 
+        first = slice(0, R)
+        every = slice(0, P)
+
         k_raw = tile("k_raw", [P, 4, N], F32)
+        q0_raw = [tile("q0_raw%d" % b, [P, 4, P], F32) for b in range(2)]
         q_raw = [tile("q_raw%d" % h, [P, 4, HALF], F32) for h in range(2)]
         v_raw = tile("v_raw", [P, 4, D], F32)
         kb_sb = tile("kb_sb", [P, 4], F32)
         t_sb = tile("t_sb", [P, 4], F32)
         gn_sb = tile("gn_sb", [P, D], F32)
         q_view = qT.rearrange("h (p j) n -> (h p) j n", j=4)
-        nc.sync.dma_start(out=k_raw[0:R], in_=kT[0].rearrange("(p j) n -> p j n", j=4))
-        nc.scalar.dma_start(out=q_raw[0][:], in_=q_view[:, :, 0:HALF])
-        nc.sync.dma_start(out=kb_sb[:], in_=kb.rearrange("(s r) o -> s (r o)", r=4))
+        nc.sync.dma_start(out=q0_raw[0][first], in_=q_view[first, :, 0:P])
+        nc.sync.dma_start(out=k_raw[first], in_=kT[0].rearrange("(p j) n -> p j n", j=4))
+        nc.scalar.dma_start(out=kb_sb[:], in_=kb.rearrange("(s r) o -> s (r o)", r=4))
+        nc.sync.dma_start(out=q0_raw[1][first], in_=q_view[first, :, P:HALF])
         nc.sync.dma_start(out=q_raw[1][:], in_=q_view[:, :, HALF:NQ])
         nc.sync.dma_start(out=t_sb[:], in_=t.rearrange("(s r) o -> s (r o)", r=4))
+        nc.sync.dma_start(out=q_raw[0][:], in_=q_view[:, :, 0:HALF])
         nc.sync.dma_start(out=v_raw[:], in_=v[0].rearrange("(s r) e -> s r e", r=4))
-        nc.sync.dma_start(out=gn_sb[:], in_=gn)
 
         k_pk = [[packed("k_pk%d_%d" % (g, a), 256) for a in range(2)] for g in range(H)]
-        q_pk = [packed("q_pk%d" % h, 256) for h in range(2)]
-        v_pk = packed("v_pk", 128)
+        q0_pk = [packed("q0_pk%d" % b, P) for b in range(2)]
+        q_pk = [packed("q_pk%d" % h, HALF) for h in range(2)]
+        v_pk = packed("v_pk", P)
         for a in range(2):
-            nc.vector.memset(k_pk[0][a][0:R, 256:320].bitcast(I32), 0)
+            nc.vector.memset(k_pk[0][a][first, 256:320].bitcast(I32), 0)
 
         k_bf = [tile("k_bf%d" % a, [P, 2, P, 4], BF16) for a in range(2)]
-        q_bf = [tile("q_bf%d" % h, [P, HALF * 4], BF16) for h in range(2)]
+        q0_bf = [tile("q0_bf%d" % b, [P, P * 4], BF16) for b in range(2)]
+        q_bf = [tile("q_bf%d" % h, [P, 2, P, 4], BF16) for h in range(2)]
         v_bf = tile("v_bf", [P, D * 4], BF16)
 
         def k_round(a):
             return dict(
-                out=k_bf[a][0:R].rearrange("p x s j -> p s j x"),
-                in_=k_raw[0:R].rearrange("p j (s r) -> p s j r", r=4)[:, :, :, 2 * a : 2 * a + 2],
+                out=k_bf[a][first].rearrange("p x s j -> p s j x"),
+                in_=k_raw[first].rearrange("p j (s r) -> p s j r", r=4)[:, :, :, 2 * a : 2 * a + 2],
             )
 
+        def q_round(h):
+            return dict(out=q_bf[h][:].rearrange("p b m j -> p m j b"), in_=q_raw[h][:].rearrange("p j (m b) -> p m j b", b=2))
+
         def interleave(dst, src):
-            return dict(
-                out=dst[:].rearrange("p (c i j) -> p c j i", i=4, j=4),
-                in_=src[:].rearrange("p j (c i) -> p c j i", i=4),
-            )
+            return dict(out=dst.rearrange("p (c i j) -> p c j i", i=4, j=4), in_=src.rearrange("p j (c i) -> p c j i", i=4))
+
+        def quant(pk, words, rows, c0, n, src):
+            nc.vector.quantize_mx(out=codes(pk, words, rows, c0, n), scales=scales(pk, words, rows, c0, n), in_=src)
 
         def k_quant(r):
             a, x = divmod(r, 2)
-            rows = slice(0, R)
-            nc.vector.quantize_mx(
-                out=codes(k_pk[0][a], 256, rows, P * x, P),
-                scales=scales(k_pk[0][a], 256, rows, P * x, P),
-                in_=k_bf[a][0:R, x].rearrange("p s j -> p (s j)"),
-            )
+            quant(k_pk[0][a], 256, first, P * x, P, k_bf[a][first, x].rearrange("p s j -> p (s j)"))
 
-        def quant(pk, words, src):
-            rows = slice(0, P)
-            nc.vector.quantize_mx(out=codes(pk, words, rows, 0, words), scales=scales(pk, words, rows, 0, words), in_=src)
+        def q_quant(h):
+            quant(q_pk[h], HALF, every, 0, HALF, q_bf[h][:].rearrange("p b m j -> p (b m j)"))
 
         def k_share(g, a):
-            nc.sync.dma_start(out=k_pk[g][a][R * g : R * g + R].bitcast(I32), in_=k_pk[0][a][0:R].bitcast(I32))
+            nc.sync.dma_start(out=k_pk[g][a][R * g : R * g + R].bitcast(I32), in_=k_pk[0][a][first].bitcast(I32))
 
         s_bank = [ps.tile([P, 512], F32, name="s_bank%d" % b) for b in range(5)]
         y_bank = [ps.tile([P, 512], F32, name="y_bank%d" % b) for b in range(3)]
 
         def bank_of(u, a):
             g = UNITS[u][0]
-            return s_bank[a] if g == 0 else s_bank[g + 1]
+            return s_bank[1 - a] if g == 0 else s_bank[g + 1]
 
-        def y_of(u):
-            return y_bank[(u // 2) % 3][:, HALF * (u % 2) : HALF * (u % 2) + HALF]
+        def y_of(j, n=1):
+            bank, slot = divmod(j, 4) if j < 12 else divmod(j - 12, 2)
+            return y_bank[bank][:, P * slot : P * (slot + n)]
 
-        sig1 = [tile("sig1_%d" % u, [P, 4, HALF], F32) for u in range(8)]
-        prob = [[tile("prob%d_%d" % (u, b), [P, 4, P], F32) for b in range(2)] for u in range(8)]
-        w_bf = [[tile("w_bf%d_%d" % (u, b), [P, 4 * P], BF16) for b in range(2)] for u in range(8)]
-        w_pk = [[packed("w_pk%d_%d" % (u, b), 128) for b in range(2)] for u in range(8)]
+        sig1 = {u: tile("sig1_%d" % u, [P, 4, HALF], F32) for u in range(1, 6)}
+        sig1_block = {j: tile("sig1b_%d" % j, [P, 4, P], F32) for j in (0, 1, 12, 13, 14, 15)}
+        prob = [tile("prob%d" % j, [P, 4, P], F32) for j in range(16)]
+        w_bf = [tile("w_bf%d" % j, [P, 4 * P], BF16) for j in range(16)]
+        w_pk = [packed("w_pk%d" % j, P) for j in range(16)]
         res = [tile("res%d" % u, [P, 2, D], F32) for u in range(8)]
 
-        def fill(u, a):
-            g, h = UNITS[u]
+        def sig1_of(j):
+            return sig1_block[j][:] if j in sig1_block else sig1[j // 2][:, :, P * (j % 2) : P * (j % 2) + P]
+
+        def score(j, r, dst):
+            g, h, b = BLOCKS[j]
             rows = slice(R * g, R * g + R)
+            a, x = divmod(r, 2)
+            pk, words, c0 = (q0_pk[b], P, 0) if j < 2 else (q_pk[h], HALF, P * b)
+            nc.tensor.matmul_mx(
+                out=dst,
+                lhsT=codes(k_pk[g][a], 256, rows, P * x, P),
+                lhsT_scale=scales(k_pk[g][a], 256, rows, P * x, P),
+                rhs=codes(pk, words, rows, c0, P),
+                rhs_scale=scales(pk, words, rows, c0, P),
+                start=True,
+                stop=True,
+            )
+
+        def cap(dst, src, r):
+            nc.scalar.activation(out=dst, in_=src, func=ACT.Sigmoid, bias=kb_sb[:, r : r + 1])
+
+        def fill(u, a):
             for x in range(2):
                 for b in range(2):
                     c0 = HALF * x + P * b
-                    nc.tensor.matmul_mx(
-                        out=bank_of(u, a)[:, c0 : c0 + P],
-                        lhsT=codes(k_pk[g][a], 256, rows, P * x, P),
-                        lhsT_scale=scales(k_pk[g][a], 256, rows, P * x, P),
-                        rhs=codes(q_pk[h], 256, rows, P * b, P),
-                        rhs_scale=scales(q_pk[h], 256, rows, P * b, P),
-                        start=True,
-                        stop=True,
-                    )
+                    score(2 * u + b, 2 * a + x, bank_of(u, a)[:, c0 : c0 + P])
 
         def inner(u, a):
             for x in range(2):
-                r = 2 * a + x
-                nc.scalar.activation(
-                    out=sig1[u][:, r, :], in_=bank_of(u, a)[:, HALF * x : HALF * x + HALF], func=ACT.Sigmoid, bias=kb_sb[:, r : r + 1]
-                )
+                cap(sig1[u][:, 2 * a + x, :], bank_of(u, a)[:, HALF * x : HALF * x + HALF], 2 * a + x)
 
-        def outer(u, b):
-            nc.scalar.activation(out=prob[u][b][:], in_=sig1[u][:, :, P * b : P * b + P], func=ACT.Sigmoid, scale=4.0, bias=-2.0)
+        def fill_block(j, bank):
+            for r in range(4):
+                score(j, r, bank[:, P * r : P * r + P])
 
-        def weigh(u, b):
+        def inner_block(j, bank):
+            for r in range(4):
+                cap(sig1_of(j)[:, r, :], bank[:, P * r : P * r + P], r)
+
+        def outer(j):
+            nc.scalar.activation(out=prob[j][:], in_=sig1_of(j), func=ACT.Sigmoid, scale=4.0, bias=-2.0)
+
+        def weigh(j):
             nc.vector.tensor_tensor(
-                out=w_bf[u][b][:].rearrange("p (c i r) -> p c r i", i=4, r=4),
-                in0=prob[u][b][:].rearrange("p r (c i) -> p c r i", i=4),
+                out=w_bf[j][:].rearrange("p (c i r) -> p c r i", i=4, r=4),
+                in0=prob[j][:].rearrange("p r (c i) -> p c r i", i=4),
                 in1=t_sb[:].unsqueeze(1).unsqueeze(3).to_broadcast([P, P // 4, 4, 4]),
                 op=ALU.mult,
             )
 
-        def w_quant(u, b):
-            quant(w_pk[u][b], 128, w_bf[u][b][:])
+        def w_quant(j):
+            quant(w_pk[j], P, every, 0, P, w_bf[j][:])
 
-        def second(u, b):
-            rows = slice(0, P)
+        def second(j):
             nc.tensor.matmul_mx(
-                out=y_of(u)[:, P * b : P * b + P],
-                lhsT=codes(w_pk[u][b], 128, rows, 0, P),
-                lhsT_scale=scales(w_pk[u][b], 128, rows, 0, P),
-                rhs=codes(v_pk, 128, rows, 0, P),
-                rhs_scale=scales(v_pk, 128, rows, 0, P),
+                out=y_of(j),
+                lhsT=codes(w_pk[j], P, every, 0, P),
+                lhsT_scale=scales(w_pk[j], P, every, 0, P),
+                rhs=codes(v_pk, P, every, 0, P),
+                rhs_scale=scales(v_pk, P, every, 0, P),
                 start=True,
                 stop=True,
             )
 
         st_early = tile("st_early", [P, 2 * EARLY, 3], F32)
-        st_late = tile("st_late", [P, 2 * (7 - EARLY), 3], F32)
+        st_late = tile("st_late", [P, 2 * (6 - EARLY), 3], F32)
 
         def stats(u):
             st, i = (st_early, u) if u < EARLY else (st_late, u - EARLY)
             nc.vector.bn_stats(
-                out=st[:, 2 * i : 2 * i + 2, :].rearrange("p b s -> p (b s)"), in_=y_of(u).rearrange("p (b e) -> p e b", b=2)
+                out=st[:, 2 * i : 2 * i + 2, :].rearrange("p b s -> p (b s)"), in_=y_of(2 * u, 2).rearrange("p (b e) -> p e b", b=2)
             )
 
-        def finish(u, b, rstd):
+        def finish(j, rstd, gain):
             nc.vector.scalar_tensor_tensor(
-                out=res[u][:, b, :], in0=y_of(u)[:, P * b : P * b + P], scalar=rstd, in1=gn_sb[:], op0=ALU.mult, op1=ALU.mult
+                out=res[j // 2][:, j % 2, :], in0=y_of(j), scalar=rstd, in1=gain[:], op0=ALU.mult, op1=ALU.mult
             )
+
+        def rows_of(g, h):
+            return out[g, HALF * h : HALF * h + HALF, :]
 
         def store(u):
             g, h = UNITS[u]
-            nc.sync.dma_start(out=out[g, HALF * h : HALF * h + HALF, :].rearrange("(b p) e -> p b e", b=2), in_=res[u][:])
+            order = "(b p) e -> p b e" if u == 0 else "(p b) e -> p b e"
+            nc.sync.dma_start(out=rows_of(g, h).rearrange(order, b=2), in_=res[u][:])
 
-        def small(name, n, dtype=F32):
-            return tile(name, [P, n], dtype)
+        def store_block(j):
+            g, h, b = BLOCKS[j]
+            nc.sync.dma_start(out=rows_of(g, h).rearrange("(p b) e -> p b e", b=2)[:, b, :], in_=res[j // 2][:, j % 2, :])
 
         ne = 2 * EARLY
-        m2, ms, xh = small("m2", ne), small("ms", ne), small("xh", ne)
+        m2, var, neg = small("m2", ne), small("var", ne), small("neg", ne)
         guess = small("guess", ne, I32)
+        y0 = guess[:].bitcast(F32)
+        a1, b1, y1, a2, b2, h2, h3, root = [small("chain%d" % i, ne) for i in range(8)]
+        gn_early = tile("gn_early", [P, D], F32)
+
+        def moments():
+            nc.vector.scalar_tensor_tensor(
+                out=m2[:], in0=st_early[:, :, 1], scalar=-1.0, in1=st_early[:, :, 1], op0=ALU.mult, op1=ALU.mult
+            )
+            nc.vector.tensor_scalar(out=var[:], in0=st_early[:, :, 2], scalar1=-1.0 / D, scalar2=-EPS, op0=ALU.mult, op1=ALU.add)
+
+        def mul(dst, x, y):
+            return lambda: nc.vector.tensor_tensor(out=dst[:], in0=x, in1=y, op=ALU.mult)
+
+        def fused(dst, x, op, c, y):
+            return lambda: nc.vector.scalar_tensor_tensor(out=dst[:], in0=x, scalar=c, in1=y, op0=op, op1=ALU.mult)
+
         chain = [
-            lambda: nc.vector.tensor_tensor(out=m2[:], in0=st_early[:, :, 1], in1=st_early[:, :, 1], op=ALU.mult),
-            lambda: nc.vector.scalar_tensor_tensor(
-                out=ms[:], in0=st_early[:, :, 2], scalar=1.0 / D, in1=m2[:], op0=ALU.mult, op1=ALU.add
-            ),
-            lambda: nc.vector.tensor_scalar(out=xh[:], in0=ms[:], scalar1=EPS, scalar2=-0.5, op0=ALU.add, op1=ALU.mult),
+            moments,
+            lambda: nc.vector.tensor_tensor(out=neg[:], in0=m2[:], in1=var[:], op=ALU.add),
             lambda: nc.vector.tensor_scalar(
-                out=guess[:], in0=xh[:].bitcast(I32), scalar1=-0.5, scalar2=GUESS, op0=ALU.mult, op1=ALU.add
+                out=guess[:], in0=neg[:].bitcast(I32), scalar1=-0.5, scalar2=GUESS, op0=ALU.mult, op1=ALU.add
             ),
+            mul(a1, y0, y0),
+            mul(b1, a1[:], neg[:]),
+            fused(y1, b1[:], ALU.add, STEP_A, y0),
+            mul(a2, y1[:], y1[:]),
+            fused(b2, a2[:], ALU.mult, STEP_K * STEP_K, neg[:]),
+            fused(h2, b2[:], ALU.add, 21.0 / 5.0, b2[:]),
+            fused(h3, h2[:], ALU.add, 7.0, b2[:]),
+            fused(root, h3[:], ALU.add, 7.0, y1[:]),
         ]
 
-        def newton(i, root):
-            a, b, nxt = small("na%d" % i, ne), small("nb%d" % i, ne), small("nr%d" % i, ne)
-            chain.extend(
-                [
-                    lambda: nc.vector.tensor_tensor(out=a[:], in0=root, in1=root, op=ALU.mult),
-                    lambda: nc.vector.tensor_tensor(out=b[:], in0=a[:], in1=xh[:], op=ALU.mult),
-                    lambda: nc.vector.scalar_tensor_tensor(out=nxt[:], in0=b[:], scalar=1.5, in1=root, op0=ALU.add, op1=ALU.mult),
-                ]
-            )
-            return nxt[:]
-
-        root = guess[:].bitcast(F32)
-        for i in range(3):
-            root = newton(i, root)
-
         def link():
-            if chain:
-                chain[0]()
-                chain.remove(chain[0])
+            chain[0]()
+            chain.remove(chain[0])
 
+        def finish_early(u):
+            for j in (2 * u, 2 * u + 1):
+                finish(j, root[:, j : j + 1], gn_early)
+            store(u)
+
+        warm = small("warm", 2)
+        nc.gpsimd.memset(warm[:, 0:1], 0.0)
+        nc.scalar.activation(out=warm[:, 1:2], in_=warm[:, 0:1], func=ACT.Sigmoid)
+        nc.vector.tensor_copy(**interleave(q0_bf[0][first], q0_raw[0][first]))
+        quant(q0_pk[0], P, first, 0, P, q0_bf[0][first])
         nc.vector.tensor_copy(**k_round(0))
-        nc.vector.tensor_copy(**interleave(q_bf[0], q_raw[0]))
+        nc.scalar.copy(**k_round(1))
+        nc.vector.tensor_copy(**interleave(q0_bf[1][first], q0_raw[1][first]))
         k_quant(0)
         k_quant(1)
-        quant(q_pk[0], 256, q_bf[0][:])
-        nc.vector.tensor_copy(**k_round(1))
-        nc.vector.tensor_copy(**interleave(q_bf[1], q_raw[1]))
+        quant(q0_pk[1], P, first, 0, P, q0_bf[1][first])
         k_quant(2)
         k_quant(3)
-        quant(q_pk[1], 256, q_bf[1][:])
-        nc.vector.tensor_copy(**interleave(v_bf, v_raw))
         for g in range(1, H):
             for a in range(2):
                 k_share(g, a)
-        fill(0, 0)
-        fill(0, 1)
-        inner(0, 0)
-        inner(0, 1)
+        nc.sync.dma_start(out=gn_sb[:], in_=gn)
+        nc.vector.tensor_copy(**q_round(1))
+        q_quant(1)
+        nc.vector.tensor_copy(**q_round(0))
+        for a in range(2):
+            for r in (2 * a, 2 * a + 1):
+                score(0, r, s_bank[a][:, P * r : P * r + P])
+            for r in (2 * a, 2 * a + 1):
+                cap(sig1_of(0)[:, r, :], s_bank[a][:, P * r : P * r + P], r)
+        fill_block(1, s_bank[0])
         fill(1, 0)
+        outer(0)
+        inner_block(1, s_bank[0])
 
-        for u in range(7):
-            if u == 0:
-                outer(0, 0)
-            inner(u + 1, 0)
-            fill(u + 1, 1)
-            if u + 2 < 8:
+        for u in range(6):
+            if 0 < u < 4:
                 fill(u + 2, 0)
-            if u > 0:
-                second(u - 1, 0)
-                second(u - 1, 1)
-                outer(u, 0)
-            outer(u, 1)
-            inner(u + 1, 1)
-            weigh(u, 0)
+            if u == 4:
+                fill_block(12, s_bank[3])
+            if u < 5:
+                inner(u + 1, 0)
+                fill(u + 1, 1)
+            else:
+                inner_block(12, s_bank[3])
+                fill_block(13, s_bank[4])
             if u == 0:
-                quant(v_pk, 128, v_bf[:])
+                q_quant(0)
+                fill(2, 0)
+            if u > 0:
+                second(2 * u - 2)
+                second(2 * u - 1)
+                outer(2 * u)
+            outer(2 * u + 1)
+            if u < 5:
+                inner(u + 1, 1)
+            weigh(2 * u)
+            if u == 0:
+                nc.vector.tensor_copy(**interleave(v_bf[:], v_raw[:]))
+                quant(v_pk, P, every, 0, P, v_bf[:])
             if u > EARLY:
                 link()
             if u > 0:
                 stats(u - 1)
             if u > EARLY:
                 link()
-            weigh(u, 1)
-            for b in range(2):
-                if u >= EARLY:
-                    link()
-                w_quant(u, b)
+            weigh(2 * u + 1)
             if u >= EARLY:
                 link()
-        for u in range(2):
-            for b in range(2):
-                finish(u, b, root[:, 2 * u + b : 2 * u + b + 1])
+            w_quant(2 * u)
+            if u == EARLY:
+                link()
+            w_quant(2 * u + 1)
+            if u in (3, 4):
+                link()
+            if u == 4:
+                link()
+            if u == 1:
+                nc.vector.tensor_scalar(out=gn_early[:], in0=gn_sb[:], scalar1=0.3125 * STEP_K, scalar2=None, op0=ALU.mult)
+
+        nl = 2 * (6 - EARLY)
+        m2l, ssl, rl = small("m2l", nl), small("ssl", nl), small("rl", nl)
+        finish_early(0)
+        fill_block(14, s_bank[3])
+        inner_block(13, s_bank[4])
+        fill_block(15, s_bank[4])
+        second(10)
+        second(11)
+        outer(12)
+        inner_block(14, s_bank[3])
+        outer(13)
+        inner_block(15, s_bank[4])
+        outer(14)
+        outer(15)
+        weigh(12)
+        stats(5)
+        w_quant(12)
+        weigh(13)
+        nc.vector.tensor_tensor(out=m2l[:], in0=st_late[:, :, 1], in1=st_late[:, :, 1], op=ALU.mult)
+        finish(4, root[:, 4:5], gn_early)
+        w_quant(13)
+        weigh(14)
+        nc.vector.scalar_tensor_tensor(out=ssl[:], in0=m2l[:], scalar=float(D), in1=st_late[:, :, 2], op0=ALU.mult, op1=ALU.add)
+        weigh(15)
+        w_quant(14)
+        finish(5, root[:, 5:6], gn_early)
+        w_quant(15)
+        store(2)
+        for j in range(12, 16):
+            second(j)
+        finish_early(1)
+
+        def roots(dst, src):
+            nc.scalar.activation(out=dst, in_=src, func=ACT.Abs_reciprocal_sqrt, scale=1.0 / D, bias=EPS)
+
+        ss_last = [small("ss_last%d" % i, 2) for i in range(2)]
+        r_last = [small("r_last%d" % i, 2) for i in range(2)]
+        sq = tile("sq", [P, 4, D], F32)
+
+        def squares(j):
+            i, b = divmod(j - 12, 2)
+            nc.scalar.activation(out=sq[:, j - 12, :], in_=y_of(j), func=ACT.Square, accum_out=ss_last[i][:, b : b + 1])
+
+        def finish_late(u):
+            for j in (2 * u, 2 * u + 1):
+                finish(j, rl[:, j - ne : j - ne + 1], gn_sb)
             store(u)
 
-        second(6, 0)
-        second(6, 1)
-        outer(7, 0)
-        outer(7, 1)
-        weigh(7, 0)
-        weigh(7, 1)
-        w_quant(7, 0)
-        w_quant(7, 1)
-        second(7, 0)
-        second(7, 1)
-        nl = 2 * (7 - EARLY)
-        m2l, ssl, rl = small("m2l", nl), small("ssl", nl), small("rl", nl)
-        stats(6)
-        finish(2, 0, root[:, 4:5])
-        nc.vector.tensor_tensor(out=m2l[:], in0=st_late[:, :, 1], in1=st_late[:, :, 1], op=ALU.mult)
-        finish(2, 1, root[:, 5:6])
-        nc.vector.scalar_tensor_tensor(out=ssl[:], in0=m2l[:], scalar=float(D), in1=st_late[:, :, 2], op0=ALU.mult, op1=ALU.add)
-        store(2)
-        finish(3, 0, root[:, 6:7])
-        finish(3, 1, root[:, 7:8])
-        store(3)
-        nc.scalar.activation(out=rl[:], in_=ssl[:], func=ACT.Abs_reciprocal_sqrt, scale=1.0 / D, bias=EPS)
-        ss7, r7 = small("ss7", 2), small("r7", 2)
-        sq = tile("sq", [P, 2, D], F32)
-        for b in range(2):
-            nc.scalar.activation(out=sq[:, b, :], in_=y_of(7)[:, P * b : P * b + P], func=ACT.Square, accum_out=ss7[:, b : b + 1])
-        nc.scalar.activation(out=r7[:], in_=ss7[:], func=ACT.Abs_reciprocal_sqrt, scale=1.0 / D, bias=EPS)
-        for u in range(EARLY, 7):
+        def finish_last(i):
             for b in range(2):
-                finish(u, b, rl[:, 2 * (u - EARLY) + b : 2 * (u - EARLY) + b + 1])
-            store(u)
-        for b in range(2):
-            finish(7, b, r7[:, b : b + 1])
-        store(7)
+                finish(12 + 2 * i + b, r_last[i][:, b : b + 1], gn_sb)
+                store_block(12 + 2 * i + b)
+
+        roots(rl[:], ssl[:])
+        for j in (12, 14, 15, 13):
+            squares(j)
+        roots(r_last[1][:], ss_last[1][:])
+        roots(r_last[0][:], ss_last[0][:])
+        for u in (4, 5, 3):
+            finish_late(u)
+        finish_last(1)
+        finish_last(0)

@@ -1,3 +1,4 @@
+import math
 from contextlib import ExitStack
 
 import concourse.mybir as mybir
@@ -20,8 +21,8 @@ HALF = 256
 EPS = 256 * 1e-5
 GUESS = float(0x5F1FFFF9 - 2**30)
 STEP_A, STEP_K = 2.38924456, 0.703952253
-UNITS = [(0, 0), (0, 1), (1, 0), (2, 0), (1, 1), (3, 0)]
-BLOCKS = [(g, h, b) for g, h in UNITS for b in range(2)] + [(g, 1, b) for b in range(2) for g in (2, 3)]
+UNITS = [(0, 0), (0, 1), (1, 1), (2, 1), (1, 0), (3, 1)]
+BLOCKS = [(g, h, b) for g, h in UNITS for b in range(2)] + [(g, 0, b) for b in range(2) for g in (2, 3)]
 EARLY = 3
 
 
@@ -51,31 +52,31 @@ def tile_rows_a_sigmoid_kb_cap_onorm_kernel(tc, qT, kT, t, v, kb, gn, out):
         every = slice(0, P)
 
         k_raw = tile("k_raw", [P, 4, N], F32)
-        q0_raw = [tile("q0_raw%d" % b, [P, 4, P], F32) for b in range(2)]
+        q0_raw = [tile("q0_raw%d" % i, [P, 4, n], F32) for i, n in enumerate((P, P, HALF))]
         q_raw = [tile("q_raw%d" % h, [P, 4, HALF], F32) for h in range(2)]
         v_raw = tile("v_raw", [P, 4, D], F32)
         kb_sb = tile("kb_sb", [P, 4], F32)
         t_sb = tile("t_sb", [P, 4], F32)
         gn_sb = tile("gn_sb", [P, D], F32)
         q_view = qT.rearrange("h (p j) n -> (h p) j n", j=4)
-        nc.sync.dma_start(out=q0_raw[0][first], in_=q_view[first, :, 0:P])
         nc.sync.dma_start(out=k_raw[first], in_=kT[0].rearrange("(p j) n -> p j n", j=4))
+        nc.sync.dma_start(out=q0_raw[0][first], in_=q_view[first, :, 0:P])
         nc.scalar.dma_start(out=kb_sb[:], in_=kb.rearrange("(s r) o -> s (r o)", r=4))
         nc.sync.dma_start(out=q0_raw[1][first], in_=q_view[first, :, P:HALF])
-        nc.sync.dma_start(out=q_raw[1][:], in_=q_view[:, :, HALF:NQ])
+        nc.sync.dma_start(out=q0_raw[2][first], in_=q_view[first, :, HALF:NQ])
         nc.sync.dma_start(out=t_sb[:], in_=t.rearrange("(s r) o -> s (r o)", r=4))
-        nc.sync.dma_start(out=q_raw[0][:], in_=q_view[:, :, 0:HALF])
+        nc.sync.dma_start(out=q_raw[1][:], in_=q_view[:, :, HALF:NQ])
         nc.sync.dma_start(out=v_raw[:], in_=v[0].rearrange("(s r) e -> s r e", r=4))
 
         k_pk = [[packed("k_pk%d_%d" % (g, a), 256) for a in range(2)] for g in range(H)]
-        q0_pk = [packed("q0_pk%d" % b, P) for b in range(2)]
+        q0_pk = [packed("q0_pk%d" % b, P) for b in range(4)]
         q_pk = [packed("q_pk%d" % h, HALF) for h in range(2)]
         v_pk = packed("v_pk", P)
         for a in range(2):
             nc.vector.memset(k_pk[0][a][first, 256:320].bitcast(I32), 0)
 
         k_bf = [tile("k_bf%d" % a, [P, 2, P, 4], BF16) for a in range(2)]
-        q0_bf = [tile("q0_bf%d" % b, [P, P * 4], BF16) for b in range(2)]
+        q0_bf = [tile("q0_bf%d" % i, [P, n * 4], BF16) for i, n in enumerate((P, P, HALF))]
         q_bf = [tile("q_bf%d" % h, [P, 2, P, 4], BF16) for h in range(2)]
         v_bf = tile("v_bf", [P, D * 4], BF16)
 
@@ -89,7 +90,7 @@ def tile_rows_a_sigmoid_kb_cap_onorm_kernel(tc, qT, kT, t, v, kb, gn, out):
             return dict(out=q_bf[h][:].rearrange("p b m j -> p m j b"), in_=q_raw[h][:].rearrange("p j (m b) -> p m j b", b=2))
 
         def interleave(dst, src):
-            return dict(out=dst.rearrange("p (c i j) -> p c j i", i=4, j=4), in_=src.rearrange("p j (c i) -> p c j i", i=4))
+            return dict(out=dst.rearrange("p (c i j) -> p c j i", i=2, j=4), in_=src.rearrange("p j (c i) -> p c j i", i=2))
 
         def quant(pk, words, rows, c0, n, src):
             nc.vector.quantize_mx(out=codes(pk, words, rows, c0, n), scales=scales(pk, words, rows, c0, n), in_=src)
@@ -129,7 +130,7 @@ def tile_rows_a_sigmoid_kb_cap_onorm_kernel(tc, qT, kT, t, v, kb, gn, out):
             g, h, b = BLOCKS[j]
             rows = slice(R * g, R * g + R)
             a, x = divmod(r, 2)
-            pk, words, c0 = (q0_pk[b], P, 0) if j < 2 else (q_pk[h], HALF, P * b)
+            pk, words, c0 = (q0_pk[j], P, 0) if g == 0 else (q_pk[h], HALF, P * b)
             nc.tensor.matmul_mx(
                 out=dst,
                 lhsT=codes(k_pk[g][a], 256, rows, P * x, P),
@@ -166,9 +167,9 @@ def tile_rows_a_sigmoid_kb_cap_onorm_kernel(tc, qT, kT, t, v, kb, gn, out):
 
         def weigh(j):
             nc.vector.tensor_tensor(
-                out=w_bf[j][:].rearrange("p (c i r) -> p c r i", i=4, r=4),
-                in0=prob[j][:].rearrange("p r (c i) -> p c r i", i=4),
-                in1=t_sb[:].unsqueeze(1).unsqueeze(3).to_broadcast([P, P // 4, 4, 4]),
+                out=w_bf[j][:].rearrange("p (c i r) -> p c r i", i=2, r=4),
+                in0=prob[j][:].rearrange("p r (c i) -> p c r i", i=2),
+                in1=t_sb[:].unsqueeze(1).unsqueeze(3).to_broadcast([P, P // 2, 4, 2]),
                 op=ALU.mult,
             )
 
@@ -205,7 +206,7 @@ def tile_rows_a_sigmoid_kb_cap_onorm_kernel(tc, qT, kT, t, v, kb, gn, out):
 
         def store(u):
             g, h = UNITS[u]
-            order = "(b p) e -> p b e" if u == 0 else "(p b) e -> p b e"
+            order = "(b p) e -> p b e" if g == 0 else "(p b) e -> p b e"
             nc.sync.dma_start(out=rows_of(g, h).rearrange(order, b=2), in_=res[u][:])
 
         def store_block(j):
@@ -213,17 +214,11 @@ def tile_rows_a_sigmoid_kb_cap_onorm_kernel(tc, qT, kT, t, v, kb, gn, out):
             nc.sync.dma_start(out=rows_of(g, h).rearrange("(p b) e -> p b e", b=2)[:, b, :], in_=res[j // 2][:, j % 2, :])
 
         ne = 2 * EARLY
-        m2, var, neg = small("m2", ne), small("var", ne), small("neg", ne)
+        m2, neg = small("m2", ne), small("neg", ne)
         guess = small("guess", ne, I32)
         y0 = guess[:].bitcast(F32)
         a1, b1, y1, a2, b2, h2, h3, root = [small("chain%d" % i, ne) for i in range(8)]
         gn_early = tile("gn_early", [P, D], F32)
-
-        def moments():
-            nc.vector.scalar_tensor_tensor(
-                out=m2[:], in0=st_early[:, :, 1], scalar=-1.0, in1=st_early[:, :, 1], op0=ALU.mult, op1=ALU.mult
-            )
-            nc.vector.tensor_scalar(out=var[:], in0=st_early[:, :, 2], scalar1=-1.0 / D, scalar2=-EPS, op0=ALU.mult, op1=ALU.add)
 
         def mul(dst, x, y):
             return lambda: nc.vector.tensor_tensor(out=dst[:], in0=x, in1=y, op=ALU.mult)
@@ -232,8 +227,10 @@ def tile_rows_a_sigmoid_kb_cap_onorm_kernel(tc, qT, kT, t, v, kb, gn, out):
             return lambda: nc.vector.scalar_tensor_tensor(out=dst[:], in0=x, scalar=c, in1=y, op0=op, op1=ALU.mult)
 
         chain = [
-            moments,
-            lambda: nc.vector.tensor_tensor(out=neg[:], in0=m2[:], in1=var[:], op=ALU.add),
+            fused(m2, st_early[:, :, 1], ALU.mult, -float(D), st_early[:, :, 1]),
+            lambda: nc.vector.scalar_tensor_tensor(
+                out=neg[:], in0=m2[:], scalar=-D * EPS, in1=st_early[:, :, 2], op0=ALU.add, op1=ALU.subtract
+            ),
             lambda: nc.vector.tensor_scalar(
                 out=guess[:], in0=neg[:].bitcast(I32), scalar1=-0.5, scalar2=GUESS, op0=ALU.mult, op1=ALU.add
             ),
@@ -259,23 +256,22 @@ def tile_rows_a_sigmoid_kb_cap_onorm_kernel(tc, qT, kT, t, v, kb, gn, out):
         warm = small("warm", 2)
         nc.gpsimd.memset(warm[:, 0:1], 0.0)
         nc.scalar.activation(out=warm[:, 1:2], in_=warm[:, 0:1], func=ACT.Sigmoid)
-        nc.vector.tensor_copy(**interleave(q0_bf[0][first], q0_raw[0][first]))
-        quant(q0_pk[0], P, first, 0, P, q0_bf[0][first])
-        nc.vector.tensor_copy(**k_round(0))
-        nc.scalar.copy(**k_round(1))
-        nc.vector.tensor_copy(**interleave(q0_bf[1][first], q0_raw[1][first]))
+        for a in range(2):
+            nc.vector.tensor_copy(**k_round(a))
+            nc.scalar.copy(**interleave(q0_bf[a][first], q0_raw[a][first]))
         k_quant(0)
-        k_quant(1)
+        quant(q0_pk[0], P, first, 0, P, q0_bf[0][first])
+        for r in range(1, 4):
+            k_quant(r)
         quant(q0_pk[1], P, first, 0, P, q0_bf[1][first])
-        k_quant(2)
-        k_quant(3)
         for g in range(1, H):
             for a in range(2):
                 k_share(g, a)
+        nc.sync.dma_start(out=q_raw[0][:], in_=q_view[:, :, 0:HALF])
         nc.sync.dma_start(out=gn_sb[:], in_=gn)
-        nc.vector.tensor_copy(**q_round(1))
-        q_quant(1)
-        nc.vector.tensor_copy(**q_round(0))
+        nc.vector.tensor_copy(**interleave(q0_bf[2][first], q0_raw[2][first]))
+        for b in range(2):
+            quant(q0_pk[2 + b], P, first, 0, P, q0_bf[2][first, 4 * P * b : 4 * P * (b + 1)])
         for a in range(2):
             for r in (2 * a, 2 * a + 1):
                 score(0, r, s_bank[a][:, P * r : P * r + P])
@@ -285,6 +281,12 @@ def tile_rows_a_sigmoid_kb_cap_onorm_kernel(tc, qT, kT, t, v, kb, gn, out):
         fill(1, 0)
         outer(0)
         inner_block(1, s_bank[0])
+        nc.vector.tensor_copy(**q_round(1))
+        weigh(0)
+        q_quant(1)
+        nc.vector.tensor_copy(**interleave(v_bf[:], v_raw[:]))
+        w_quant(0)
+        quant(v_pk, P, every, 0, P, v_bf[:])
 
         for u in range(6):
             if 0 < u < 4:
@@ -298,7 +300,6 @@ def tile_rows_a_sigmoid_kb_cap_onorm_kernel(tc, qT, kT, t, v, kb, gn, out):
                 inner_block(12, s_bank[3])
                 fill_block(13, s_bank[4])
             if u == 0:
-                q_quant(0)
                 fill(2, 0)
             if u > 0:
                 second(2 * u - 2)
@@ -307,10 +308,8 @@ def tile_rows_a_sigmoid_kb_cap_onorm_kernel(tc, qT, kT, t, v, kb, gn, out):
             outer(2 * u + 1)
             if u < 5:
                 inner(u + 1, 1)
-            weigh(2 * u)
-            if u == 0:
-                nc.vector.tensor_copy(**interleave(v_bf[:], v_raw[:]))
-                quant(v_pk, P, every, 0, P, v_bf[:])
+            if u > 0:
+                weigh(2 * u)
             if u > EARLY:
                 link()
             if u > 0:
@@ -320,16 +319,21 @@ def tile_rows_a_sigmoid_kb_cap_onorm_kernel(tc, qT, kT, t, v, kb, gn, out):
             weigh(2 * u + 1)
             if u >= EARLY:
                 link()
-            w_quant(2 * u)
+            if u > 0:
+                w_quant(2 * u)
             if u == EARLY:
                 link()
+            if u == 0:
+                nc.vector.tensor_copy(**q_round(0))
             w_quant(2 * u + 1)
+            if u == 0:
+                q_quant(0)
             if u in (3, 4):
                 link()
             if u == 4:
                 link()
             if u == 1:
-                nc.vector.tensor_scalar(out=gn_early[:], in0=gn_sb[:], scalar1=0.3125 * STEP_K, scalar2=None, op0=ALU.mult)
+                nc.vector.tensor_scalar(out=gn_early[:], in0=gn_sb[:], scalar1=0.3125 * STEP_K * math.sqrt(D), scalar2=None, op0=ALU.mult)
 
         nl = 2 * (6 - EARLY)
         m2l, ssl, rl = small("m2l", nl), small("ssl", nl), small("rl", nl)

@@ -19,11 +19,8 @@ P = 128
 R = 32
 HALF = 256
 EPS = 256 * 1e-5
-GUESS = float(0x5F1FFFF9 - 2**30)
-STEP_A, STEP_K = 2.38924456, 0.703952253
 UNITS = [(0, 0), (0, 1), (1, 1), (2, 1), (1, 0), (3, 1)]
 BLOCKS = [(g, h, b) for g, h in UNITS for b in range(2)] + [(g, 0, b) for b in range(2) for g in (2, 3)]
-EARLY = 3
 
 
 def tile_rows_a_sigmoid_kb_cap_onorm_kernel(tc, qT, kT, t, v, kb, gn, out):
@@ -119,8 +116,8 @@ def tile_rows_a_sigmoid_kb_cap_onorm_kernel(tc, qT, kT, t, v, kb, gn, out):
         sig1 = {u: tile("sig1_%d" % u, [P, 4, HALF], F32) for u in range(1, 6)}
         sig1_block = {j: tile("sig1b_%d" % j, [P, 4, P], F32) for j in (0, 1, 12, 13, 14, 15)}
         prob = [tile("prob%d" % j, [P, 4, P], F32) for j in range(16)]
-        w_bf = [tile("w_bf%d" % j, [P, 4 * P], BF16) for j in range(16)]
-        w_pk = [packed("w_pk%d" % j, P) for j in range(16)]
+        w_bf = [tile("w_bf%d" % u, [P, 2, 4 * P], BF16) for u in range(8)]
+        w_pk = [packed("w_pk%d" % u, HALF) for u in range(8)]
         res = [tile("res%d" % u, [P, 2, D], F32) for u in range(8)]
 
         def sig1_of(j):
@@ -167,33 +164,35 @@ def tile_rows_a_sigmoid_kb_cap_onorm_kernel(tc, qT, kT, t, v, kb, gn, out):
 
         def weigh(j):
             nc.vector.tensor_tensor(
-                out=w_bf[j][:].rearrange("p (c i r) -> p c r i", i=2, r=4),
+                out=w_bf[j // 2][:, j % 2, :].rearrange("p (c i r) -> p c r i", i=2, r=4),
                 in0=prob[j][:].rearrange("p r (c i) -> p c r i", i=2),
                 in1=t_sb[:].unsqueeze(1).unsqueeze(3).to_broadcast([P, P // 2, 4, 2]),
                 op=ALU.mult,
             )
 
         def w_quant(j):
-            quant(w_pk[j], P, every, 0, P, w_bf[j][:])
+            quant(w_pk[j // 2], HALF, every, P * (j % 2), P, w_bf[j // 2][:, j % 2, :])
+
+        def w_quant_unit(u):
+            quant(w_pk[u], HALF, every, 0, HALF, w_bf[u][:].rearrange("p b n -> p (b n)"))
 
         def second(j):
             nc.tensor.matmul_mx(
                 out=y_of(j),
-                lhsT=codes(w_pk[j], P, every, 0, P),
-                lhsT_scale=scales(w_pk[j], P, every, 0, P),
+                lhsT=codes(w_pk[j // 2], HALF, every, P * (j % 2), P),
+                lhsT_scale=scales(w_pk[j // 2], HALF, every, P * (j % 2), P),
                 rhs=codes(v_pk, P, every, 0, P),
                 rhs_scale=scales(v_pk, P, every, 0, P),
                 start=True,
                 stop=True,
             )
 
-        st_early = tile("st_early", [P, 2 * EARLY, 3], F32)
-        st_late = tile("st_late", [P, 2 * (6 - EARLY), 3], F32)
+        st = [tile("st%d" % c, [P, 2 if c < 4 else 4, 3], F32) for c in range(5)]
 
         def stats(u):
-            st, i = (st_early, u) if u < EARLY else (st_late, u - EARLY)
+            i = max(u - 4, 0)
             nc.vector.bn_stats(
-                out=st[:, 2 * i : 2 * i + 2, :].rearrange("p b s -> p (b s)"), in_=y_of(2 * u, 2).rearrange("p (b e) -> p e b", b=2)
+                out=st[min(u, 4)][:, 2 * i : 2 * i + 2, :].rearrange("p b s -> p (b s)"), in_=y_of(2 * u, 2).rearrange("p (b e) -> p e b", b=2)
             )
 
         def finish(j, rstd, gain):
@@ -213,44 +212,27 @@ def tile_rows_a_sigmoid_kb_cap_onorm_kernel(tc, qT, kT, t, v, kb, gn, out):
             g, h, b = BLOCKS[j]
             nc.sync.dma_start(out=rows_of(g, h).rearrange("(p b) e -> p b e", b=2)[:, b, :], in_=res[j // 2][:, j % 2, :])
 
-        ne = 2 * EARLY
-        m2, neg = small("m2", ne), small("neg", ne)
-        guess = small("guess", ne, I32)
-        y0 = guess[:].bitcast(F32)
-        a1, b1, y1, a2, b2, h2, h3, root = [small("chain%d" % i, ne) for i in range(8)]
-        gn_early = tile("gn_early", [P, D], F32)
+        power = small("power", 2)
+        nc.gpsimd.memset(power[:], -0.5)
+        gn_root = tile("gn_root", [P, D], F32)
+        groups = [(u, 2) for u in range(4)] + [(4, 4)]
+        m2, ssum, root = [[small("%s%d" % (name, c), n) for c, n in groups] for name in ("m2", "ssum", "root")]
 
-        def mul(dst, x, y):
-            return lambda: nc.vector.tensor_tensor(out=dst[:], in0=x, in1=y, op=ALU.mult)
+        def mean_part(c):
+            nc.vector.scalar_tensor_tensor(
+                out=m2[c][:], in0=st[c][:, :, 1], scalar=float(D), in1=st[c][:, :, 1], op0=ALU.mult, op1=ALU.mult
+            )
 
-        def fused(dst, x, op, c, y):
-            return lambda: nc.vector.scalar_tensor_tensor(out=dst[:], in0=x, scalar=c, in1=y, op0=op, op1=ALU.mult)
+        def square_sum(c):
+            nc.vector.scalar_tensor_tensor(out=ssum[c][:], in0=m2[c][:], scalar=D * EPS, in1=st[c][:, :, 2], op0=ALU.add, op1=ALU.add)
 
-        chain = [
-            fused(m2, st_early[:, :, 1], ALU.mult, -float(D), st_early[:, :, 1]),
-            lambda: nc.vector.scalar_tensor_tensor(
-                out=neg[:], in0=m2[:], scalar=-D * EPS, in1=st_early[:, :, 2], op0=ALU.add, op1=ALU.subtract
-            ),
-            lambda: nc.vector.tensor_scalar(
-                out=guess[:], in0=neg[:].bitcast(I32), scalar1=-0.5, scalar2=GUESS, op0=ALU.mult, op1=ALU.add
-            ),
-            mul(a1, y0, y0),
-            mul(b1, a1[:], neg[:]),
-            fused(y1, b1[:], ALU.add, STEP_A, y0),
-            mul(a2, y1[:], y1[:]),
-            fused(b2, a2[:], ALU.mult, STEP_K * STEP_K, neg[:]),
-            fused(h2, b2[:], ALU.add, 21.0 / 5.0, b2[:]),
-            fused(h3, h2[:], ALU.add, 7.0, b2[:]),
-            fused(root, h3[:], ALU.add, 7.0, y1[:]),
-        ]
-
-        def link():
-            chain[0]()
-            chain.remove(chain[0])
+        def power_roots(c):
+            nc.gpsimd.tensor_tensor(out=root[c][:], in0=ssum[c][:], in1=power[:], op=ALU.pow)
 
         def finish_early(u):
             for j in (2 * u, 2 * u + 1):
-                finish(j, root[:, j : j + 1], gn_early)
+                c = min(u, 4)
+                finish(j, root[c][:, j - 2 * c : j - 2 * c + 1], gn_root)
             store(u)
 
         warm = small("warm", 2)
@@ -308,36 +290,27 @@ def tile_rows_a_sigmoid_kb_cap_onorm_kernel(tc, qT, kT, t, v, kb, gn, out):
             outer(2 * u + 1)
             if u < 5:
                 inner(u + 1, 1)
-            if u > 0:
-                weigh(2 * u)
-            if u > EARLY:
-                link()
-            if u > 0:
-                stats(u - 1)
-            if u > EARLY:
-                link()
-            weigh(2 * u + 1)
-            if u >= EARLY:
-                link()
-            if u > 0:
-                w_quant(2 * u)
-            if u == EARLY:
-                link()
             if u == 0:
+                weigh(1)
                 nc.vector.tensor_copy(**q_round(0))
-            w_quant(2 * u + 1)
-            if u == 0:
+                w_quant(1)
                 q_quant(0)
-            if u in (3, 4):
-                link()
-            if u == 4:
-                link()
+                continue
+            weigh(2 * u)
             if u == 1:
-                nc.vector.tensor_scalar(out=gn_early[:], in0=gn_sb[:], scalar1=0.3125 * STEP_K * math.sqrt(D), scalar2=None, op0=ALU.mult)
+                weigh(3)
+                nc.vector.tensor_scalar(out=gn_root[:], in0=gn_sb[:], scalar1=math.sqrt(D), scalar2=None, op0=ALU.mult)
+                w_quant_unit(u)
+            else:
+                mean_part(u - 2)
+                weigh(2 * u + 1)
+                square_sum(u - 2)
+                w_quant_unit(u)
+                power_roots(u - 2)
+            stats(u - 1)
+            if u >= 3:
+                finish_early(u - 3)
 
-        nl = 2 * (6 - EARLY)
-        m2l, ssl, rl = small("m2l", nl), small("ssl", nl), small("rl", nl)
-        finish_early(0)
         fill_block(14, s_bank[3])
         inner_block(13, s_bank[4])
         fill_block(15, s_bank[4])
@@ -352,20 +325,19 @@ def tile_rows_a_sigmoid_kb_cap_onorm_kernel(tc, qT, kT, t, v, kb, gn, out):
         weigh(12)
         stats(5)
         w_quant(12)
+        mean_part(4)
         weigh(13)
-        nc.vector.tensor_tensor(out=m2l[:], in0=st_late[:, :, 1], in1=st_late[:, :, 1], op=ALU.mult)
-        finish(4, root[:, 4:5], gn_early)
+        square_sum(4)
+        finish(6, root[3][:, 0:1], gn_root)
         w_quant(13)
         weigh(14)
-        nc.vector.scalar_tensor_tensor(out=ssl[:], in0=m2l[:], scalar=float(D), in1=st_late[:, :, 2], op0=ALU.mult, op1=ALU.add)
+        finish(7, root[3][:, 1:2], gn_root)
+        store(3)
         weigh(15)
         w_quant(14)
-        finish(5, root[:, 5:6], gn_early)
         w_quant(15)
-        store(2)
         for j in range(12, 16):
             second(j)
-        finish_early(1)
 
         def roots(dst, src):
             nc.scalar.activation(out=dst, in_=src, func=ACT.Abs_reciprocal_sqrt, scale=1.0 / D, bias=EPS)
@@ -378,22 +350,18 @@ def tile_rows_a_sigmoid_kb_cap_onorm_kernel(tc, qT, kT, t, v, kb, gn, out):
             i, b = divmod(j - 12, 2)
             nc.scalar.activation(out=sq[:, j - 12, :], in_=y_of(j), func=ACT.Square, accum_out=ss_last[i][:, b : b + 1])
 
-        def finish_late(u):
-            for j in (2 * u, 2 * u + 1):
-                finish(j, rl[:, j - ne : j - ne + 1], gn_sb)
-            store(u)
-
         def finish_last(i):
             for b in range(2):
                 finish(12 + 2 * i + b, r_last[i][:, b : b + 1], gn_sb)
                 store_block(12 + 2 * i + b)
 
-        roots(rl[:], ssl[:])
-        for j in (12, 14, 15, 13):
+        nc.scalar.activation(out=root[4][:], in_=ssum[4][:], func=ACT.Abs_reciprocal_sqrt)
+        for j in (12, 13, 14):
             squares(j)
-        roots(r_last[1][:], ss_last[1][:])
         roots(r_last[0][:], ss_last[0][:])
-        for u in (4, 5, 3):
-            finish_late(u)
-        finish_last(1)
+        squares(15)
+        roots(r_last[1][:], ss_last[1][:])
+        finish_early(4)
+        finish_early(5)
         finish_last(0)
+        finish_last(1)

import math
from contextlib import ExitStack

import concourse.mybir as mybir

H, D, NQ, N = 4, 128, 512, 512
FLOPS = 2 * 2 * H * NQ * N * D

F32 = mybir.dt.float32
BF16 = mybir.dt.bfloat16
I32 = mybir.dt.int32
U32 = mybir.dt.uint32
U8 = mybir.dt.uint8
FP8X4 = mybir.dt.float8_e4m3fn_x4
ACT = mybir.ActivationFunctionType
ALU = mybir.AluOpType

P = 128
R = 32
HALF = 256
EPS = 256 * 1e-5
UNITS = [(0, 0), (0, 1), (1, 1), (2, 1), (1, 0), (3, 1)]
BLOCKS = [(g, h, b) for g, h in UNITS for b in range(2)] + [(g, 0, b) for b in range(2) for g in (2, 3)]


def tile_rows_a_sigmoid_kb_cap_onorm_kernel(tc, qT, kT, t, v, kb, gn, out):
    nc = tc.nc
    with ExitStack() as ctx:
        sb = ctx.enter_context(tc.tile_pool(name="sb", bufs=1))
        ps = ctx.enter_context(tc.psum_pool(name="ps", bufs=1))
        ctx.enter_context(tc.manual_schedule())

        def tile(name, shape, dtype):
            return sb.tile(shape, dtype, name=name, align_bytes=64)

        def small(name, n, dtype=F32):
            return tile(name, [P, n], dtype)

        def packed(name, words):
            return tile(name, [P, words + words // 4], U32)

        def codes(pk, words, rows, c0, n):
            return pk[rows, c0 : c0 + n].bitcast(FP8X4)

        def scales(pk, words, rows, c0, n):
            return pk[rows, words + c0 // 4 : words + (c0 + n) // 4].bitcast(U8)

        first = slice(0, R)
        every = slice(0, P)

        k_raw = tile("k_raw", [P, 4, N], F32)
        q0_raw = [tile("q0_raw%d" % i, [P, 4, n], F32) for i, n in enumerate((P, P, HALF))]
        q_raw = [tile("q_raw%d" % h, [P, 4, HALF], F32) for h in range(2)]
        v_raw = tile("v_raw", [P, 4, D], F32)
        kb_sb = tile("kb_sb", [P, 4], F32)
        t_sb = tile("t_sb", [P, 4], F32)
        gn_sb = tile("gn_sb", [P, D], F32)
        q_view = qT.rearrange("h (p j) n -> (h p) j n", j=4)
        nc.sync.dma_start(out=k_raw[first], in_=kT[0].rearrange("(p j) n -> p j n", j=4))
        nc.sync.dma_start(out=q0_raw[0][first], in_=q_view[first, :, 0:P])
        nc.scalar.dma_start(out=kb_sb[:], in_=kb.rearrange("(s r) o -> s (r o)", r=4))
        nc.sync.dma_start(out=q0_raw[1][first], in_=q_view[first, :, P:HALF])
        nc.sync.dma_start(out=q0_raw[2][first], in_=q_view[first, :, HALF:NQ])
        nc.sync.dma_start(out=t_sb[:], in_=t.rearrange("(s r) o -> s (r o)", r=4))
        nc.sync.dma_start(out=q_raw[1][:], in_=q_view[:, :, HALF:NQ])
        nc.sync.dma_start(out=v_raw[:], in_=v[0].rearrange("(s r) e -> s r e", r=4))

        k_pk = [[packed("k_pk%d_%d" % (g, a), 256) for a in range(2)] for g in range(H)]
        q0_pk = [packed("q0_pk%d" % b, P) for b in range(4)]
        q_pk = [packed("q_pk%d" % h, HALF) for h in range(2)]
        v_pk = packed("v_pk", P)
        for a in range(2):
            nc.vector.memset(k_pk[0][a][first, 256:320].bitcast(I32), 0)

        k_bf = [tile("k_bf%d" % a, [P, 2, P, 4], BF16) for a in range(2)]
        q0_bf = [tile("q0_bf%d" % i, [P, n * 4], BF16) for i, n in enumerate((P, P, HALF))]
        q_bf = [tile("q_bf%d" % h, [P, 2, P, 4], BF16) for h in range(2)]
        v_bf = tile("v_bf", [P, D * 4], BF16)

        def k_round(a):
            return dict(
                out=k_bf[a][first].rearrange("p x s j -> p s j x"),
                in_=k_raw[first].rearrange("p j (s r) -> p s j r", r=4)[:, :, :, 2 * a : 2 * a + 2],
            )

        def q_round(h):
            return dict(out=q_bf[h][:].rearrange("p b m j -> p m j b"), in_=q_raw[h][:].rearrange("p j (m b) -> p m j b", b=2))

        def interleave(dst, src):
            return dict(out=dst.rearrange("p (c i j) -> p c j i", i=2, j=4), in_=src.rearrange("p j (c i) -> p c j i", i=2))

        def quant(pk, words, rows, c0, n, src):
            nc.vector.quantize_mx(out=codes(pk, words, rows, c0, n), scales=scales(pk, words, rows, c0, n), in_=src)

        def k_quant(r):
            a, x = divmod(r, 2)
            quant(k_pk[0][a], 256, first, P * x, P, k_bf[a][first, x].rearrange("p s j -> p (s j)"))

        def q_quant(h):
            quant(q_pk[h], HALF, every, 0, HALF, q_bf[h][:].rearrange("p b m j -> p (b m j)"))

        def k_share(g, a):
            nc.sync.dma_start(out=k_pk[g][a][R * g : R * g + R].bitcast(I32), in_=k_pk[0][a][first].bitcast(I32))

        s_bank = [ps.tile([P, 512], F32, name="s_bank%d" % b) for b in range(5)]
        y_bank = [ps.tile([P, 512], F32, name="y_bank%d" % b) for b in range(3)]

        def bank_of(u, a):
            g = UNITS[u][0]
            return s_bank[1 - a] if g == 0 else s_bank[g + 1]

        def y_of(j, n=1):
            bank, slot = divmod(j, 4) if j < 12 else divmod(j - 12, 2)
            return y_bank[bank][:, P * slot : P * (slot + n)]

        sig1 = {u: tile("sig1_%d" % u, [P, 4, HALF], F32) for u in range(1, 6)}
        sig1_block = {j: tile("sig1b_%d" % j, [P, 4, P], F32) for j in (0, 1, 12, 13, 14, 15)}
        prob = [tile("prob%d" % j, [P, 4, P], F32) for j in range(16)]
        w_bf = [tile("w_bf%d" % u, [P, 2, 4 * P], BF16) for u in range(8)]
        w_pk = [packed("w_pk%d" % u, HALF) for u in range(8)]
        res = [tile("res%d" % u, [P, 2, D], F32) for u in range(8)]

        def sig1_of(j):
            return sig1_block[j][:] if j in sig1_block else sig1[j // 2][:, :, P * (j % 2) : P * (j % 2) + P]

        def score(j, r, dst):
            g, h, b = BLOCKS[j]
            rows = slice(R * g, R * g + R)
            a, x = divmod(r, 2)
            pk, words, c0 = (q0_pk[j], P, 0) if g == 0 else (q_pk[h], HALF, P * b)
            nc.tensor.matmul_mx(
                out=dst,
                lhsT=codes(k_pk[g][a], 256, rows, P * x, P),
                lhsT_scale=scales(k_pk[g][a], 256, rows, P * x, P),
                rhs=codes(pk, words, rows, c0, P),
                rhs_scale=scales(pk, words, rows, c0, P),
                start=True,
                stop=True,
            )

        def cap(dst, src, r):
            nc.scalar.activation(out=dst, in_=src, func=ACT.Sigmoid, bias=kb_sb[:, r : r + 1])

        def fill(u, a):
            for x in range(2):
                for b in range(2):
                    c0 = HALF * x + P * b
                    score(2 * u + b, 2 * a + x, bank_of(u, a)[:, c0 : c0 + P])

        def inner(u, a):
            for x in range(2):
                cap(sig1[u][:, 2 * a + x, :], bank_of(u, a)[:, HALF * x : HALF * x + HALF], 2 * a + x)

        def fill_block(j, bank):
            for r in range(4):
                score(j, r, bank[:, P * r : P * r + P])

        def inner_block(j, bank):
            for r in range(4):
                cap(sig1_of(j)[:, r, :], bank[:, P * r : P * r + P], r)

        def outer(j):
            nc.scalar.activation(out=prob[j][:], in_=sig1_of(j), func=ACT.Sigmoid, scale=4.0, bias=-2.0)

        def weigh(j):
            nc.vector.tensor_tensor(
                out=w_bf[j // 2][:, j % 2, :].rearrange("p (c i r) -> p c r i", i=2, r=4),
                in0=prob[j][:].rearrange("p r (c i) -> p c r i", i=2),
                in1=t_sb[:].unsqueeze(1).unsqueeze(3).to_broadcast([P, P // 2, 4, 2]),
                op=ALU.mult,
            )

        def w_quant(j):
            quant(w_pk[j // 2], HALF, every, P * (j % 2), P, w_bf[j // 2][:, j % 2, :])

        def w_quant_unit(u):
            quant(w_pk[u], HALF, every, 0, HALF, w_bf[u][:].rearrange("p b n -> p (b n)"))

        def second(j):
            nc.tensor.matmul_mx(
                out=y_of(j),
                lhsT=codes(w_pk[j // 2], HALF, every, P * (j % 2), P),
                lhsT_scale=scales(w_pk[j // 2], HALF, every, P * (j % 2), P),
                rhs=codes(v_pk, P, every, 0, P),
                rhs_scale=scales(v_pk, P, every, 0, P),
                start=True,
                stop=True,
            )

        st = [tile("st%d" % c, [P, 2 if c < 4 else 4, 3], F32) for c in range(5)]

        def stats(u):
            i = max(u - 4, 0)
            nc.vector.bn_stats(
                out=st[min(u, 4)][:, 2 * i : 2 * i + 2, :].rearrange("p b s -> p (b s)"), in_=y_of(2 * u, 2).rearrange("p (b e) -> p e b", b=2)
            )

        def finish(j, rstd, gain):
            nc.vector.scalar_tensor_tensor(
                out=res[j // 2][:, j % 2, :], in0=y_of(j), scalar=rstd, in1=gain[:], op0=ALU.mult, op1=ALU.mult
            )

        def rows_of(g, h):
            return out[g, HALF * h : HALF * h + HALF, :]

        def store(u):
            g, h = UNITS[u]
            order = "(b p) e -> p b e" if g == 0 else "(p b) e -> p b e"
            nc.sync.dma_start(out=rows_of(g, h).rearrange(order, b=2), in_=res[u][:])

        def store_block(j):
            g, h, b = BLOCKS[j]
            nc.sync.dma_start(out=rows_of(g, h).rearrange("(p b) e -> p b e", b=2)[:, b, :], in_=res[j // 2][:, j % 2, :])

        power = small("power", 2)
        nc.gpsimd.memset(power[:], -0.5)
        gn_root = tile("gn_root", [P, D], F32)
        groups = [(u, 2) for u in range(4)] + [(4, 4)]
        m2, ssum, root = [[small("%s%d" % (name, c), n) for c, n in groups] for name in ("m2", "ssum", "root")]

        def mean_part(c):
            nc.vector.scalar_tensor_tensor(
                out=m2[c][:], in0=st[c][:, :, 1], scalar=float(D), in1=st[c][:, :, 1], op0=ALU.mult, op1=ALU.mult
            )

        def square_sum(c):
            nc.vector.scalar_tensor_tensor(out=ssum[c][:], in0=m2[c][:], scalar=D * EPS, in1=st[c][:, :, 2], op0=ALU.add, op1=ALU.add)

        def power_roots(c):
            nc.gpsimd.tensor_tensor(out=root[c][:], in0=ssum[c][:], in1=power[:], op=ALU.pow)

        def finish_early(u):
            for j in (2 * u, 2 * u + 1):
                c = min(u, 4)
                finish(j, root[c][:, j - 2 * c : j - 2 * c + 1], gn_root)
            store(u)

        warm = small("warm", 2)
        nc.gpsimd.memset(warm[:, 0:1], 0.0)
        nc.scalar.activation(out=warm[:, 1:2], in_=warm[:, 0:1], func=ACT.Sigmoid)
        for a in range(2):
            nc.vector.tensor_copy(**k_round(a))
            nc.scalar.copy(**interleave(q0_bf[a][first], q0_raw[a][first]))
        k_quant(0)
        quant(q0_pk[0], P, first, 0, P, q0_bf[0][first])
        for r in range(1, 4):
            k_quant(r)
        quant(q0_pk[1], P, first, 0, P, q0_bf[1][first])
        for g in range(1, H):
            for a in range(2):
                k_share(g, a)
        nc.sync.dma_start(out=q_raw[0][:], in_=q_view[:, :, 0:HALF])
        nc.sync.dma_start(out=gn_sb[:], in_=gn)
        nc.vector.tensor_copy(**interleave(q0_bf[2][first], q0_raw[2][first]))
        for b in range(2):
            quant(q0_pk[2 + b], P, first, 0, P, q0_bf[2][first, 4 * P * b : 4 * P * (b + 1)])
        for a in range(2):
            for r in (2 * a, 2 * a + 1):
                score(0, r, s_bank[a][:, P * r : P * r + P])
            for r in (2 * a, 2 * a + 1):
                cap(sig1_of(0)[:, r, :], s_bank[a][:, P * r : P * r + P], r)
        fill_block(1, s_bank[0])
        fill(1, 0)
        outer(0)
        inner_block(1, s_bank[0])
        nc.vector.tensor_copy(**q_round(1))
        weigh(0)
        q_quant(1)
        nc.vector.tensor_copy(**interleave(v_bf[:], v_raw[:]))
        w_quant(0)
        quant(v_pk, P, every, 0, P, v_bf[:])

        for u in range(6):
            if 0 < u < 4:
                fill(u + 2, 0)
            if u == 4:
                fill_block(12, s_bank[3])
            if u < 5:
                inner(u + 1, 0)
                fill(u + 1, 1)
            else:
                inner_block(12, s_bank[3])
                fill_block(13, s_bank[4])
            if u == 0:
                fill(2, 0)
            if u > 0:
                second(2 * u - 2)
                second(2 * u - 1)
                outer(2 * u)
            outer(2 * u + 1)
            if u < 5:
                inner(u + 1, 1)
            if u == 0:
                weigh(1)
                nc.vector.tensor_copy(**q_round(0))
                w_quant(1)
                q_quant(0)
                continue
            weigh(2 * u)
            if u == 1:
                weigh(3)
                nc.vector.tensor_scalar(out=gn_root[:], in0=gn_sb[:], scalar1=math.sqrt(D), scalar2=None, op0=ALU.mult)
                w_quant_unit(u)
            else:
                mean_part(u - 2)
                weigh(2 * u + 1)
                square_sum(u - 2)
                w_quant_unit(u)
                power_roots(u - 2)
            stats(u - 1)
            if u >= 3:
                finish_early(u - 3)

        fill_block(14, s_bank[3])
        inner_block(13, s_bank[4])
        fill_block(15, s_bank[4])
        second(10)
        second(11)
        outer(12)
        inner_block(14, s_bank[3])
        outer(13)
        inner_block(15, s_bank[4])
        outer(14)
        outer(15)
        weigh(12)
        stats(5)
        w_quant(12)
        mean_part(4)
        weigh(13)
        square_sum(4)
        finish(6, root[3][:, 0:1], gn_root)
        w_quant(13)
        weigh(14)
        finish(7, root[3][:, 1:2], gn_root)
        store(3)
        weigh(15)
        w_quant(14)
        w_quant(15)
        for j in range(12, 16):
            second(j)

        def roots(dst, src):
            nc.scalar.activation(out=dst, in_=src, func=ACT.Abs_reciprocal_sqrt, scale=1.0 / D, bias=EPS)

        ss_last = [small("ss_last%d" % i, 2) for i in range(2)]
        r_last = [small("r_last%d" % i, 2) for i in range(2)]
        sq = tile("sq", [P, 4, D], F32)

        def squares(j):
            i, b = divmod(j - 12, 2)
            nc.scalar.activation(out=sq[:, j - 12, :], in_=y_of(j), func=ACT.Square, accum_out=ss_last[i][:, b : b + 1])

        def finish_last(i):
            for b in range(2):
                finish(12 + 2 * i + b, r_last[i][:, b : b + 1], gn_sb)
                store_block(12 + 2 * i + b)

        nc.scalar.activation(out=root[4][:], in_=ssum[4][:], func=ACT.Abs_reciprocal_sqrt)
        for j in (12, 13, 14):
            squares(j)
        roots(r_last[0][:], ss_last[0][:])
        squares(15)
        roots(r_last[1][:], ss_last[1][:])
        finish_early(4)
        finish_early(5)
        finish_last(0)
        finish_last(1)
